import numpy as np
import ml_dtypes


def mxq(x, axis, fmt="e4m3"):
    dtype, down = {"e4m3": (ml_dtypes.float8_e4m3fn, 7), "e5m2": (ml_dtypes.float8_e5m2, 14)}[fmt]
    v = np.moveaxis(np.asarray(x, np.float32).astype(ml_dtypes.bfloat16).astype(np.float64), axis, -1)
    blocks = v.reshape(v.shape[:-1] + (-1, 32))
    amax = np.abs(blocks).max(-1, keepdims=True)
    byte = np.maximum(np.where(amax > 0, np.frexp(amax)[1] - 1 + 127, 0) - down, 1)
    scale = np.exp2(byte - 127.0)
    codes = (blocks / scale).astype(np.float32).astype(dtype).astype(np.float64)
    return np.moveaxis((codes * scale).reshape(v.shape), -1, axis)


WIDE = False


def mx_kscale(k):
    if not WIDE:
        return np.ones(k)
    levels = np.array([10, -10, 5, -5, 0])
    if k % 512:
        return np.exp2(np.random.permutation(np.resize(levels, k // 32))).repeat(32)
    a = np.empty((k // 512, 16))
    for p in range(k // 512):
        a[p, :8] = np.random.permutation(np.resize(levels, 8))
        for g in range(8):
            far = levels[np.abs(levels - a[p, g]) >= 10]
            a[p, g + 8] = far[np.random.randint(len(far))]
    return np.exp2(a.ravel()).repeat(32)


def f64(x):
    return np.asarray(x).astype(np.float64)


def striped(idx):
    return np.tile(idx.reshape(-1, 16).T, (8, 1)).astype(np.uint16)


def unstriped(offs):
    return offs[:16].T.reshape(-1).astype(np.int64)


def striped8(idx):
    return np.concatenate([x.reshape(-1, 16).T for x in idx]).astype(np.uint16)


def runs(offs, k):
    lists = np.stack([offs[16 * r : 16 * r + 16].T.reshape(-1) for r in range(8)]).astype(np.int64)
    return lists[np.arange(k) % 512 // 64]


def pack_weight(w):
    k, n = w.shape
    w = f64(np.asarray(w, np.float32).astype(ml_dtypes.bfloat16)).reshape(k // 32, 32, n)
    amax = np.abs(w).max(1)
    byte = np.clip(np.where(amax > 0, np.frexp(amax)[1] - 1 + 127 - 7, 1), 1, 254)
    scaled = (w * np.exp2(127.0 - byte)[:, None, :]).reshape(k, n).astype(np.float32)
    words = np.ascontiguousarray(scaled.reshape(k // 512, 128, 4, n).transpose(0, 1, 3, 2)).astype(ml_dtypes.float8_e4m3fn).view(np.uint8)
    return words, np.ascontiguousarray(byte.astype(np.uint8).reshape(k // 512, 16, n))


def unpack_weight(words, scales):
    g, p, n, _ = words.shape
    vals = np.ascontiguousarray(words).view(ml_dtypes.float8_e4m3fn).astype(np.float64) * np.repeat(np.exp2(scales.astype(np.float64) - 127.0), 8, axis=1)[..., None]
    return vals.transpose(0, 1, 3, 2).reshape(g * 512, n)


def sigmoid(v):
    return 1.0 / (1.0 + np.exp(-np.maximum(v, -700.0)))

def planes(y):
    n, m = y.shape
    v = y.astype(np.float32).astype(ml_dtypes.bfloat16).astype(np.float64).reshape(n // 32, 32, m)
    top = np.abs(v).max(1)
    byte = np.clip(np.where(top > 0, np.frexp(top)[1] - 1 + 127 - 7, 1), 1, 254)
    codes = (v * np.exp2(127.0 - byte)[:, None, :]).reshape(n, m).astype(np.float32).astype(ml_dtypes.float8_e4m3fn).view(np.uint8)
    words = codes.reshape(n // 512, 128, 4, m).transpose(0, 1, 3, 2)
    return np.ascontiguousarray(words), np.ascontiguousarray(byte.astype(np.uint8).reshape(n // 512, 16, m))


K, T, S, G, H, W = 512, 1024, 256, 2048, 512, 128


def setup_inputs():
    n = np.random.standard_normal
    s = mx_kscale(K)[:, None]
    packed_xT = pack_weight(n((K, T)) * s)
    packed_dT = pack_weight(n((K, G)) / s)
    perm = np.random.permutation(S)
    return {
        "x_words": packed_xT[0],
        "x_scales": packed_xT[1],
        "d_words": packed_dT[0],
        "d_scales": packed_dT[1],
        "gs": (np.random.uniform(0.5, 1.5, (K, 1)) * s).astype(np.float32),
        "sl": np.random.uniform(1.0, 2.0, (H, 1)).astype(np.float32),
        "th": (0.5 * n((H, 1))).astype(np.float32),
        "offs": striped8(np.random.randint(0, T, (8, S))),
        "ci": striped(np.random.permutation(G)[:H]),
        "n1": striped(perm[:W]),
        "n2": striped(perm[W:]),
        "k1": striped8(np.random.randint(0, G, (8, H))),
        "n3": striped8(np.stack([np.random.permutation(S) for _ in range(8)])),
        "n4": striped8(np.stack([np.random.permutation(S) for _ in range(8)])),
    }


def reference(x_words, x_scales, d_words, d_scales, gs, sl, th, offs, ci, n1, n2, k1, n3, n4):
    d_k1 = unpack_weight(d_words, d_scales)[np.arange(K)[:, None], runs(k1, K)]
    d_ci = unpack_weight(d_words, d_scales)[:, unstriped(ci)]
    xq = unpack_weight(x_words, x_scales)[np.arange(K)[:, None], runs(offs, K)]
    s = 0.0625 * (d_ci.T @ xq)
    pa = s[:, unstriped(n1)]
    pb = s[:, unstriped(n2)]
    rb = np.maximum(pa, pb)
    ra = pa / (np.abs(pb) + 0.5)
    ds = np.zeros((H, S))
    ds[:, unstriped(n1)] = ra
    dt = ds.copy()
    dt[:, unstriped(n2)] = rb
    z = f64(gs) * dt
    h = 0.0625 * ((d_k1.T @ mxq(z, 0, "e4m3")))
    sg = sigmoid(f64(sl) * (h[np.arange(H)[:, None], runs(n3, H)] - f64(th)))
    st = h * sg
    out_0 = st - (0.5 * (st[np.arange(H)[:, None], runs(n4, H)]))
    return (out_0,) + planes(out_0)

@@ -1,0 +1,236 @@
+from contextlib import ExitStack
+
+import concourse.mybir as mybir
+
+F32 = mybir.dt.float32
+BF16 = mybir.dt.bfloat16
+I32 = mybir.dt.int32
+U32 = mybir.dt.uint32
+U16 = mybir.dt.uint16
+U8 = mybir.dt.uint8
+FP8X4 = mybir.dt.float8_e4m3fn_x4
+ALU = mybir.AluOpType
+ACT = mybir.ActivationFunctionType
+
+P = 128
+PACK = 4
+K, T, S, G, H, W = 512, 1024, 256, 2048, 512, 128
+FLOPS = 2 * 2 * K * H * S
+
+
+def tile_picked_hwqratioehp_none_po_kernel(
+    tc, x_words, x_scales, d_words, d_scales, gs, sl, th, offs, ci, n1, n2, k1, n3, n4, out_0, out_1, out_2
+):
+    nc = tc.nc
+    with ExitStack() as ctx:
+        lists = ctx.enter_context(tc.tile_pool(name="lists", bufs=1))
+        keep = ctx.enter_context(tc.tile_pool(name="keep", bufs=1))
+        psum = ctx.enter_context(tc.psum_pool(name="psum", bufs=1))
+
+        def load_list(src, name):
+            held = lists.tile(list(src.shape), U16, name=name)
+            nc.sync.dma_start(held[:], src)
+            return held
+
+        def load_rowwise(src, name):
+            held = keep.tile([P, PACK], F32, name=name)
+            nc.sync.dma_start(held[:], src.rearrange("(p t) o -> p (t o)", t=PACK))
+            return held
+
+        def load_scale_rows(window, scales):
+            rows = scales[0].bitcast(I32)
+            for e in range(2):
+                nc.sync.dma_start(window[e:P:16, :].bitcast(I32), rows[e:16:2, :])
+
+        x_bytes = keep.tile([P, T], U8, name="x_bytes")
+        d_bytes = keep.tile([P, G], U8, name="d_bytes")
+        first_scales = keep.tile([P, S + H], U8, name="first_scales", align_bytes=64)
+        nc.vector.memset(x_bytes[:].bitcast(I32), 0)
+        nc.vector.memset(d_bytes[:].bitcast(I32), 0)
+        nc.gpsimd.memset(first_scales[:].bitcast(I32), 0)
+
+        offs_l = load_list(offs, "offs_l")
+        ci_l = load_list(ci, "ci_l")
+        load_scale_rows(x_bytes, x_scales)
+        load_scale_rows(d_bytes, d_scales)
+        d_table = keep.tile([P, G], U32, name="d_table")
+        nc.sync.dma_start(d_table[:].bitcast(I32), d_words[0].rearrange("p n t -> p (n t)").bitcast(I32))
+        x_table = keep.tile([P, T], U32, name="x_table")
+        nc.sync.dma_start(x_table[:].bitcast(I32), x_words[0].rearrange("p n t -> p (n t)").bitcast(I32))
+        n1_l = load_list(n1, "n1_l")
+        n2_l = load_list(n2, "n2_l")
+        k1_l = load_list(k1, "k1_l")
+        gs_t = load_rowwise(gs, "gs_t")
+        sl_t = load_rowwise(sl, "sl_t")
+        th_t = load_rowwise(th, "th_t")
+        n3_l = load_list(n3, "n3_l")
+        n4_l = load_list(n4, "n4_l")
+
+        picked_bytes = keep.tile([P, S + H], U8, name="picked_bytes", tag="picked_bytes")
+        nc.vector.tensor_copy(picked_bytes[:, 0:S], x_bytes[:].indirect(offs_l[:]))
+        nc.vector.tensor_copy(
+            picked_bytes[:, S : S + H].rearrange("p (t m) -> p m t", t=PACK), d_bytes[:].indirect(ci_l[:])
+        )
+        for r in range(4):
+            src = 16 * (r // 2) + r % 2
+            queue = nc.sync if r % 2 == 0 else nc.scalar
+            queue.dma_start(first_scales[r:P:32, :].bitcast(I32), picked_bytes[src:P:32, :].bitcast(I32))
+
+        ci_words = keep.tile([P, H], U32, name="ci_words", tag="picked_words", align_bytes=64)
+        nc.vector.tensor_copy(ci_words[:].rearrange("p (t m) -> p m t", t=PACK), d_table[:].indirect(ci_l[:]))
+        xq_words = keep.tile([P, S], U32, name="xq_words", align_bytes=64)
+        nc.vector.tensor_copy(xq_words[:], x_table[:].indirect(offs_l[:]))
+
+        s_bank = [psum.tile([P, S], F32, name="s_bank%d" % t) for t in range(PACK)]
+        h_bank = [psum.tile([P, S], F32, name="h_bank%d" % t) for t in range(PACK)]
+        for t in range(PACK):
+            nc.tensor.matmul_mx(
+                out=s_bank[t][:],
+                lhsT=ci_words[:, P * t : P * (t + 1)].bitcast(FP8X4),
+                lhsT_scale=first_scales[:, S + P * t : S + P * (t + 1)],
+                rhs=xq_words[:].bitcast(FP8X4),
+                rhs_scale=first_scales[:, 0:S],
+                start=True,
+                stop=True,
+            )
+
+        h_and_s = [keep.tile([P, 2 * S], F32, name="h_and_s%d" % t) for t in range(PACK)]
+        pa = keep.tile([P, PACK, W], F32, name="pa")
+        pb = keep.tile([P, PACK, W], F32, name="pb")
+        rb = keep.tile([P, PACK, W], F32, name="rb")
+        ra = keep.tile([P, PACK, W], F32, name="ra")
+        flipped = keep.tile([P, PACK, W], F32, name="flipped")
+        denom = keep.tile([P, PACK, W], F32, name="denom")
+        inverse = keep.tile([P, PACK, W], F32, name="inverse")
+        dt = [keep.tile([P, S], F32, name="dt%d" % t) for t in range(PACK)]
+        z_bf16 = keep.tile([P, S, PACK], BF16, name="z_bf16", align_bytes=64)
+
+        for t in range(PACK):
+            s_t = h_and_s[t][:, S : 2 * S]
+            nc.scalar.activation(s_t, s_bank[t][:], ACT.Copy, scale=0.0625)
+            nc.scalar.activation(pb[:, t, :], s_t.indirect(n2_l[:]), ACT.Copy)
+            nc.scalar.activation(pa[:, t, :], s_t.indirect(n1_l[:]), ACT.Copy)
+
+        k1_picked_bytes = keep.tile([P, H], U8, name="k1_picked_bytes", tag="picked_bytes")
+        k1_scales = keep.tile([P, H], U8, name="k1_scales", align_bytes=64)
+        nc.vector.tensor_copy(k1_picked_bytes[:], d_bytes[:].indirect(k1_l[:]))
+
+        for t in range(PACK):
+            nc.vector.tensor_scalar(flipped[:, t, :], pb[:, t, :], -1.0, 0.5, ALU.mult, ALU.add)
+            nc.vector.tensor_tensor(rb[:, t, :], pa[:, t, :], pb[:, t, :], ALU.max)
+            nc.vector.scalar_tensor_tensor(denom[:, t, :], pb[:, t, :], 0.5, flipped[:, t, :], ALU.add, ALU.max)
+            if t == 0:
+                nc.vector.tensor_copy(
+                    k1_scales[:].rearrange("p (t m) -> p t m", t=PACK),
+                    k1_picked_bytes[:].rearrange("p (m t) -> p t m", t=PACK),
+                )
+                for r in (2, 3):
+                    nc.sync.dma_start(k1_scales[r:P:32, :].bitcast(I32), k1_scales[14 + r : P : 32, :].bitcast(I32))
+        for t in range(PACK):
+            nc.scalar.activation(dt[t][:].indirect(n2_l[:]), rb[:, t, :], ACT.Copy)
+
+        k1_picked = keep.tile([P, H], U32, name="k1_picked", tag="picked_words", align_bytes=64)
+        k1_words = keep.tile([P, H], U32, name="k1_words", align_bytes=64)
+        bias = keep.tile([P, PACK], F32, name="bias")
+
+        halves = [slice(0, S // 2), slice(S // 2, S)]
+
+        def round_z(t):
+            nc.vector.tensor_scalar(z_bf16[:, :, t], dt[t][:], gs_t[:, t : t + 1], None, ALU.mult)
+
+        for t in range(PACK):
+            nc.vector.reciprocal(inverse[:, t, :], denom[:, t, :])
+            if t > 0:
+                nc.vector.tensor_tensor(ra[:, t - 1, :], pa[:, t - 1, :], inverse[:, t - 1, :], ALU.mult)
+                nc.scalar.activation(dt[t - 1][:].indirect(n1_l[:]), ra[:, t - 1, :], ACT.Copy)
+        nc.vector.scalar_tensor_tensor(bias[:], sl_t[:], -1.0, th_t[:], ALU.mult, ALU.mult)
+        nc.vector.tensor_tensor(ra[:, PACK - 1, :], pa[:, PACK - 1, :], inverse[:, PACK - 1, :], ALU.mult)
+        nc.scalar.activation(dt[PACK - 1][:].indirect(n1_l[:]), ra[:, PACK - 1, :], ACT.Copy)
+        nc.vector.tensor_copy(k1_picked[:], d_table[:].indirect(k1_l[:]))
+        round_z(0)
+        nc.vector.tensor_copy(
+            k1_words[:].bitcast(I32).rearrange("p (t m) -> p t m", t=PACK),
+            k1_picked[:].bitcast(I32).rearrange("p (m t) -> p t m", t=PACK),
+        )
+        for t in range(1, PACK - 1):
+            round_z(t)
+        for half in halves:
+            nc.vector.tensor_scalar(z_bf16[:, half, PACK - 1], dt[PACK - 1][:, half], gs_t[:, PACK - 1 : PACK], None, ALU.mult)
+
+        z_words = keep.tile([P, S], U32, name="z_words", align_bytes=64)
+        z_scales = keep.tile([P, S], U8, name="z_scales", align_bytes=64)
+        for half in halves:
+            nc.vector.quantize_mx(
+                out=z_words[:, half].bitcast(FP8X4),
+                scales=z_scales[:, half],
+                in_=z_bf16[:, half, :].rearrange("p j t -> p (j t)"),
+            )
+        for t in range(PACK):
+            for half in halves:
+                nc.tensor.matmul_mx(
+                    out=h_bank[t][:, half],
+                    lhsT=k1_words[:, P * t : P * (t + 1)].bitcast(FP8X4),
+                    lhsT_scale=k1_scales[:, P * t : P * (t + 1)],
+                    rhs=z_words[:, half].bitcast(FP8X4),
+                    rhs_scale=z_scales[:, half],
+                    start=True,
+                    stop=True,
+                )
+
+        st_and_sg = [keep.tile([P, 2 * S], F32, name="st_and_sg%d" % t) for t in range(PACK)]
+        fetched = keep.tile([P, PACK, S], F32, name="fetched")
+        result = keep.tile([P, PACK, S], F32, name="result")
+        result_bf16 = keep.tile([P, S, PACK], BF16, name="result_bf16", align_bytes=64)
+        out_rows = out_0.rearrange("(p t) j -> p t j", t=PACK)
+
+        for t in range(PACK):
+            nc.vector.tensor_scalar(h_and_s[t][:, 0:S], h_bank[t][:], 0.0625, None, ALU.mult)
+
+        def gate(t):
+            nc.scalar.activation(
+                st_and_sg[t][:, S : 2 * S],
+                h_and_s[t][:].indirect(n3_l[:]),
+                ACT.Sigmoid,
+                bias=bias[:, t : t + 1],
+                scale=sl_t[:, t : t + 1],
+            )
+            nc.vector.tensor_tensor(st_and_sg[t][:, 0:S], h_and_s[t][:, 0:S], st_and_sg[t][:, S : 2 * S], ALU.mult)
+
+        def finish(t):
+            nc.scalar.activation(fetched[:, t, :], st_and_sg[t][:].indirect(n4_l[:]), ACT.Copy)
+            nc.vector.scalar_tensor_tensor(
+                result[:, t, :], fetched[:, t, :], -0.5, st_and_sg[t][:, 0:S], ALU.mult, ALU.add
+            )
+            nc.sync.dma_start(out_rows[:, t, :], result[:, t, :])
+            if t % 2 == 1:
+                nc.vector.tensor_copy(
+                    result_bf16[:, :, t - 1 : t + 1], result[:, t - 1 : t + 1, :].rearrange("p t j -> p j t")
+                )
+
+        gate(0)
+        for t in range(1, PACK):
+            gate(t)
+            finish(t - 1)
+
+        out_words = keep.tile([P, S], U32, name="out_words", align_bytes=64)
+        out_scales = keep.tile([P, S], U8, name="out_scales", align_bytes=64)
+        last = PACK - 1
+        for half in halves:
+            entries = n4_l[:, half.start // 16 : half.stop // 16]
+            nc.scalar.activation(fetched[:, last, half], st_and_sg[last][:].indirect(entries), ACT.Copy)
+            nc.vector.scalar_tensor_tensor(
+                result[:, last, half], fetched[:, last, half], -0.5, st_and_sg[last][:, half], ALU.mult, ALU.add
+            )
+            nc.vector.tensor_copy(
+                result_bf16[:, half, last - 1 : last + 1], result[:, last - 1 : last + 1, half].rearrange("p t j -> p j t")
+            )
+            nc.vector.quantize_mx(
+                out=out_words[:, half].bitcast(FP8X4),
+                scales=out_scales[:, half],
+                in_=result_bf16[:, half, :].rearrange("p j t -> p (j t)"),
+            )
+        nc.sync.dma_start(out_rows[:, last, :], result[:, last, :])
+        nc.sync.dma_start(out_1[0].rearrange("p n t -> p (n t)").bitcast(I32), out_words[:].bitcast(I32))
+        for q in range(4):
+            queue = nc.scalar if q % 2 == 0 else nc.sync
+            queue.dma_start(out_2[0][4 * q : 4 * q + 4, :].bitcast(I32), out_scales[32 * q : 32 * q + 4, :].bitcast(I32))

@@ -32,53 +32,47 @@ def tile_picked_hwqratioehp_none_po_kernel(
             nc.sync.dma_start(held[:], src)
             return held
 
-        def load_rowwise(src, name):
-            held = keep.tile([P, PACK], F32, name=name)
+        def load_rowwise(src, name, tag):
+            held = keep.tile([P, PACK], F32, name=name, tag=tag, align_bytes=64)
             nc.sync.dma_start(held[:], src.rearrange("(p t) o -> p (t o)", t=PACK))
             return held
 
         def load_scale_rows(window, scales):
-            rows = scales[0].bitcast(I32)
-            for e in range(2):
-                nc.sync.dma_start(window[e:P:16, :].bitcast(I32), rows[e:16:2, :])
+            nc.sync.dma_start(window[0:P:8, :].bitcast(I32), scales[0].bitcast(I32))
 
         x_bytes = keep.tile([P, T], U8, name="x_bytes")
         d_bytes = keep.tile([P, G], U8, name="d_bytes")
-        first_scales = keep.tile([P, S + H], U8, name="first_scales", align_bytes=64)
+        first_scales = keep.tile([P, S + H], U8, name="first_scales", tag="first_scales", align_bytes=64)
         nc.vector.memset(x_bytes[:].bitcast(I32), 0)
         nc.vector.memset(d_bytes[:].bitcast(I32), 0)
-        nc.gpsimd.memset(first_scales[:].bitcast(I32), 0)
+        nc.vector.memset(first_scales[:].bitcast(I32), 0)
 
         offs_l = load_list(offs, "offs_l")
         ci_l = load_list(ci, "ci_l")
+        n1_l = load_list(n1, "n1_l")
+        n2_l = load_list(n2, "n2_l")
+        k1_l = load_list(k1, "k1_l")
         load_scale_rows(x_bytes, x_scales)
         load_scale_rows(d_bytes, d_scales)
         d_table = keep.tile([P, G], U32, name="d_table")
         nc.sync.dma_start(d_table[:].bitcast(I32), d_words[0].rearrange("p n t -> p (n t)").bitcast(I32))
-        x_table = keep.tile([P, T], U32, name="x_table")
+        x_table = keep.tile([P, T], U32, name="x_table", tag="x_table")
         nc.sync.dma_start(x_table[:].bitcast(I32), x_words[0].rearrange("p n t -> p (n t)").bitcast(I32))
-        n1_l = load_list(n1, "n1_l")
-        n2_l = load_list(n2, "n2_l")
-        k1_l = load_list(k1, "k1_l")
-        gs_t = load_rowwise(gs, "gs_t")
-        sl_t = load_rowwise(sl, "sl_t")
-        th_t = load_rowwise(th, "th_t")
         n3_l = load_list(n3, "n3_l")
         n4_l = load_list(n4, "n4_l")
 
-        picked_bytes = keep.tile([P, S + H], U8, name="picked_bytes", tag="picked_bytes")
+        picked_bytes = keep.tile([P, S + H], U8, name="picked_bytes", tag="picked_bytes", align_bytes=64)
         nc.vector.tensor_copy(picked_bytes[:, 0:S], x_bytes[:].indirect(offs_l[:]))
         nc.vector.tensor_copy(
             picked_bytes[:, S : S + H].rearrange("p (t m) -> p m t", t=PACK), d_bytes[:].indirect(ci_l[:])
         )
         for r in range(4):
-            src = 16 * (r // 2) + r % 2
             queue = nc.sync if r % 2 == 0 else nc.scalar
-            queue.dma_start(first_scales[r:P:32, :].bitcast(I32), picked_bytes[src:P:32, :].bitcast(I32))
+            queue.dma_start(first_scales[r:P:32, :].bitcast(I32), picked_bytes[8 * r : P : 32, :].bitcast(I32))
 
-        ci_words = keep.tile([P, H], U32, name="ci_words", tag="picked_words", align_bytes=64)
+        ci_words = keep.tile([P, H], U32, name="ci_words", tag="ci_words", align_bytes=64)
         nc.vector.tensor_copy(ci_words[:].rearrange("p (t m) -> p m t", t=PACK), d_table[:].indirect(ci_l[:]))
-        xq_words = keep.tile([P, S], U32, name="xq_words", align_bytes=64)
+        xq_words = keep.tile([P, S], U32, name="xq_words", tag="xq_words", align_bytes=64)
         nc.vector.tensor_copy(xq_words[:], x_table[:].indirect(offs_l[:]))
 
         s_bank = [psum.tile([P, S], F32, name="s_bank%d" % t) for t in range(PACK)]
@@ -94,6 +88,10 @@ def tile_picked_hwqratioehp_none_po_kernel(
                 stop=True,
             )
 
+        gs_t = load_rowwise(gs, "gs_t", "xq_words")
+        sl_t = load_rowwise(sl, "sl_t", "ci_words")
+        th_t = load_rowwise(th, "th_t", "first_scales")
+
         h_and_s = [keep.tile([P, 2 * S], F32, name="h_and_s%d" % t) for t in range(PACK)]
         pa = keep.tile([P, PACK, W], F32, name="pa")
         pb = keep.tile([P, PACK, W], F32, name="pb")
@@ -107,29 +105,31 @@ def tile_picked_hwqratioehp_none_po_kernel(
 
         for t in range(PACK):
             s_t = h_and_s[t][:, S : 2 * S]
-            nc.scalar.activation(s_t, s_bank[t][:], ACT.Copy, scale=0.0625)
+            if t < 3:
+                nc.scalar.activation(s_t, s_bank[t][:], ACT.Copy, scale=0.0625)
+            else:
+                nc.vector.tensor_scalar(s_t, s_bank[t][:], 0.0625, None, ALU.mult)
             nc.scalar.activation(pb[:, t, :], s_t.indirect(n2_l[:]), ACT.Copy)
             nc.scalar.activation(pa[:, t, :], s_t.indirect(n1_l[:]), ACT.Copy)
 
-        k1_picked_bytes = keep.tile([P, H], U8, name="k1_picked_bytes", tag="picked_bytes")
-        k1_scales = keep.tile([P, H], U8, name="k1_scales", align_bytes=64)
+        k1_picked_bytes = keep.tile([P, H], U8, name="k1_picked_bytes")
+        k1_scales = keep.tile([P, H], U8, name="k1_scales", tag="picked_bytes", align_bytes=64)
         nc.vector.tensor_copy(k1_picked_bytes[:], d_bytes[:].indirect(k1_l[:]))
 
-        for t in range(PACK):
-            nc.vector.tensor_scalar(flipped[:, t, :], pb[:, t, :], -1.0, 0.5, ALU.mult, ALU.add)
-            nc.vector.tensor_tensor(rb[:, t, :], pa[:, t, :], pb[:, t, :], ALU.max)
-            nc.vector.scalar_tensor_tensor(denom[:, t, :], pb[:, t, :], 0.5, flipped[:, t, :], ALU.add, ALU.max)
-            if t == 0:
-                nc.vector.tensor_copy(
-                    k1_scales[:].rearrange("p (t m) -> p t m", t=PACK),
-                    k1_picked_bytes[:].rearrange("p (m t) -> p t m", t=PACK),
-                )
-                for r in (2, 3):
-                    nc.sync.dma_start(k1_scales[r:P:32, :].bitcast(I32), k1_scales[14 + r : P : 32, :].bitcast(I32))
+        nc.vector.tensor_copy(
+            k1_scales[:].rearrange("p (t m) -> p t m", t=PACK),
+            k1_picked_bytes[:].rearrange("p (m t) -> p t m", t=PACK),
+        )
+        for r in (1, 2, 3):
+            nc.sync.dma_start(k1_scales[r:P:32, :].bitcast(I32), k1_scales[8 * r : P : 32, :].bitcast(I32))
+        for pair in (slice(0, 2), slice(2, 4)):
+            nc.vector.tensor_scalar(flipped[:, pair, :], pb[:, pair, :], -1.0, 0.5, ALU.mult, ALU.add)
+            nc.vector.tensor_tensor(rb[:, pair, :], pa[:, pair, :], pb[:, pair, :], ALU.max)
+            nc.vector.scalar_tensor_tensor(denom[:, pair, :], pb[:, pair, :], 0.5, flipped[:, pair, :], ALU.add, ALU.max)
         for t in range(PACK):
             nc.scalar.activation(dt[t][:].indirect(n2_l[:]), rb[:, t, :], ACT.Copy)
 
-        k1_picked = keep.tile([P, H], U32, name="k1_picked", tag="picked_words", align_bytes=64)
+        k1_picked = keep.tile([P, H], U32, name="k1_picked", tag="x_table")
         k1_words = keep.tile([P, H], U32, name="k1_words", align_bytes=64)
         bias = keep.tile([P, PACK], F32, name="bias")
 
@@ -147,12 +147,11 @@ def tile_picked_hwqratioehp_none_po_kernel(
         nc.vector.tensor_tensor(ra[:, PACK - 1, :], pa[:, PACK - 1, :], inverse[:, PACK - 1, :], ALU.mult)
         nc.scalar.activation(dt[PACK - 1][:].indirect(n1_l[:]), ra[:, PACK - 1, :], ACT.Copy)
         nc.vector.tensor_copy(k1_picked[:], d_table[:].indirect(k1_l[:]))
-        round_z(0)
         nc.vector.tensor_copy(
             k1_words[:].bitcast(I32).rearrange("p (t m) -> p t m", t=PACK),
             k1_picked[:].bitcast(I32).rearrange("p (m t) -> p t m", t=PACK),
         )
-        for t in range(1, PACK - 1):
+        for t in range(PACK - 1):
             round_z(t)
         for half in halves:
             nc.vector.tensor_scalar(z_bf16[:, half, PACK - 1], dt[PACK - 1][:, half], gs_t[:, PACK - 1 : PACK], None, ALU.mult)
@@ -221,9 +220,11 @@ def tile_picked_hwqratioehp_none_po_kernel(
             nc.vector.scalar_tensor_tensor(
                 result[:, last, half], fetched[:, last, half], -0.5, st_and_sg[last][:, half], ALU.mult, ALU.add
             )
+        for half in halves:
             nc.vector.tensor_copy(
                 result_bf16[:, half, last - 1 : last + 1], result[:, last - 1 : last + 1, half].rearrange("p t j -> p j t")
             )
+        for half in halves:
             nc.vector.quantize_mx(
                 out=out_words[:, half].bitcast(FP8X4),
                 scales=out_scales[:, half],

@@ -105,7 +105,7 @@ def tile_picked_hwqratioehp_none_po_kernel(
 
         for t in range(PACK):
             s_t = h_and_s[t][:, S : 2 * S]
-            if t < 3:
+            if t < 2:
                 nc.scalar.activation(s_t, s_bank[t][:], ACT.Copy, scale=0.0625)
             else:
                 nc.vector.tensor_scalar(s_t, s_bank[t][:], 0.0625, None, ALU.mult)
@@ -141,15 +141,15 @@ def tile_picked_hwqratioehp_none_po_kernel(
         for t in range(PACK):
             nc.vector.reciprocal(inverse[:, t, :], denom[:, t, :])
             if t > 0:
-                nc.vector.tensor_tensor(ra[:, t - 1, :], pa[:, t - 1, :], inverse[:, t - 1, :], ALU.mult)
+                nc.gpsimd.tensor_tensor(ra[:, t - 1, :], pa[:, t - 1, :], inverse[:, t - 1, :], ALU.mult)
                 nc.scalar.activation(dt[t - 1][:].indirect(n1_l[:]), ra[:, t - 1, :], ACT.Copy)
         nc.vector.scalar_tensor_tensor(bias[:], sl_t[:], -1.0, th_t[:], ALU.mult, ALU.mult)
-        nc.vector.tensor_tensor(ra[:, PACK - 1, :], pa[:, PACK - 1, :], inverse[:, PACK - 1, :], ALU.mult)
+        nc.gpsimd.tensor_tensor(ra[:, PACK - 1, :], pa[:, PACK - 1, :], inverse[:, PACK - 1, :], ALU.mult)
         nc.scalar.activation(dt[PACK - 1][:].indirect(n1_l[:]), ra[:, PACK - 1, :], ACT.Copy)
         nc.vector.tensor_copy(k1_picked[:], d_table[:].indirect(k1_l[:]))
         nc.vector.tensor_copy(
-            k1_words[:].bitcast(I32).rearrange("p (t m) -> p t m", t=PACK),
-            k1_picked[:].bitcast(I32).rearrange("p (m t) -> p t m", t=PACK),
+            k1_words[:].bitcast(I32).rearrange("p (t c i) -> p c t i", t=PACK, i=4),
+            k1_picked[:].bitcast(I32).rearrange("p (c i t) -> p c t i", t=PACK, i=4),
         )
         for t in range(PACK - 1):
             round_z(t)

@@ -98,7 +98,7 @@ def tile_picked_hwqratioehp_none_po_kernel(
         rb = keep.tile([P, PACK, W], F32, name="rb")
         ra = keep.tile([P, PACK, W], F32, name="ra")
         flipped = keep.tile([P, PACK, W], F32, name="flipped")
-        denom = keep.tile([P, PACK, W], F32, name="denom")
+        denom = keep.tile([P, PACK, W], F32, name="denom", tag="denom", align_bytes=64)
         inverse = keep.tile([P, PACK, W], F32, name="inverse")
         dt = [keep.tile([P, S], F32, name="dt%d" % t) for t in range(PACK)]
         z_bf16 = keep.tile([P, S, PACK], BF16, name="z_bf16", align_bytes=64)
@@ -123,14 +123,14 @@ def tile_picked_hwqratioehp_none_po_kernel(
         for r in (1, 2, 3):
             nc.sync.dma_start(k1_scales[r:P:32, :].bitcast(I32), k1_scales[8 * r : P : 32, :].bitcast(I32))
         for pair in (slice(0, 2), slice(2, 4)):
-            nc.vector.tensor_scalar(flipped[:, pair, :], pb[:, pair, :], -1.0, 0.5, ALU.mult, ALU.add)
             nc.vector.tensor_tensor(rb[:, pair, :], pa[:, pair, :], pb[:, pair, :], ALU.max)
+            nc.vector.tensor_scalar(flipped[:, pair, :], pb[:, pair, :], -1.0, 0.5, ALU.mult, ALU.add)
             nc.vector.scalar_tensor_tensor(denom[:, pair, :], pb[:, pair, :], 0.5, flipped[:, pair, :], ALU.add, ALU.max)
         for t in range(PACK):
             nc.scalar.activation(dt[t][:].indirect(n2_l[:]), rb[:, t, :], ACT.Copy)
 
         k1_picked = keep.tile([P, H], U32, name="k1_picked", tag="x_table")
-        k1_words = keep.tile([P, H], U32, name="k1_words", align_bytes=64)
+        k1_words = keep.tile([P, H], U32, name="k1_words", tag="denom", align_bytes=64)
         bias = keep.tile([P, PACK], F32, name="bias")
 
         halves = [slice(0, S // 2), slice(S // 2, S)]

from contextlib import ExitStack

import concourse.mybir as mybir

F32 = mybir.dt.float32
BF16 = mybir.dt.bfloat16
I32 = mybir.dt.int32
U32 = mybir.dt.uint32
U16 = mybir.dt.uint16
U8 = mybir.dt.uint8
FP8X4 = mybir.dt.float8_e4m3fn_x4
ALU = mybir.AluOpType
ACT = mybir.ActivationFunctionType

P = 128
PACK = 4
K, T, S, G, H, W = 512, 1024, 256, 2048, 512, 128
FLOPS = 2 * 2 * K * H * S


def tile_picked_hwqratioehp_none_po_kernel(
    tc, x_words, x_scales, d_words, d_scales, gs, sl, th, offs, ci, n1, n2, k1, n3, n4, out_0, out_1, out_2
):
    nc = tc.nc
    with ExitStack() as ctx:
        lists = ctx.enter_context(tc.tile_pool(name="lists", bufs=1))
        keep = ctx.enter_context(tc.tile_pool(name="keep", bufs=1))
        psum = ctx.enter_context(tc.psum_pool(name="psum", bufs=1))

        def load_list(src, name):
            held = lists.tile(list(src.shape), U16, name=name)
            nc.sync.dma_start(held[:], src)
            return held

        def load_rowwise(src, name, tag):
            held = keep.tile([P, PACK], F32, name=name, tag=tag, align_bytes=64)
            nc.sync.dma_start(held[:], src.rearrange("(p t) o -> p (t o)", t=PACK))
            return held

        def load_scale_rows(window, scales):
            nc.sync.dma_start(window[0:P:8, :].bitcast(I32), scales[0].bitcast(I32))

        x_bytes = keep.tile([P, T], U8, name="x_bytes")
        d_bytes = keep.tile([P, G], U8, name="d_bytes")
        first_scales = keep.tile([P, S + H], U8, name="first_scales", tag="first_scales", align_bytes=64)
        nc.vector.memset(x_bytes[:].bitcast(I32), 0)
        nc.vector.memset(d_bytes[:].bitcast(I32), 0)
        nc.vector.memset(first_scales[:].bitcast(I32), 0)

        offs_l = load_list(offs, "offs_l")
        ci_l = load_list(ci, "ci_l")
        n1_l = load_list(n1, "n1_l")
        n2_l = load_list(n2, "n2_l")
        k1_l = load_list(k1, "k1_l")
        load_scale_rows(x_bytes, x_scales)
        load_scale_rows(d_bytes, d_scales)
        d_table = keep.tile([P, G], U32, name="d_table")
        nc.sync.dma_start(d_table[:].bitcast(I32), d_words[0].rearrange("p n t -> p (n t)").bitcast(I32))
        x_table = keep.tile([P, T], U32, name="x_table", tag="x_table")
        nc.sync.dma_start(x_table[:].bitcast(I32), x_words[0].rearrange("p n t -> p (n t)").bitcast(I32))
        n3_l = load_list(n3, "n3_l")
        n4_l = load_list(n4, "n4_l")

        picked_bytes = keep.tile([P, S + H], U8, name="picked_bytes", tag="picked_bytes", align_bytes=64)
        nc.vector.tensor_copy(picked_bytes[:, 0:S], x_bytes[:].indirect(offs_l[:]))
        nc.vector.tensor_copy(
            picked_bytes[:, S : S + H].rearrange("p (t m) -> p m t", t=PACK), d_bytes[:].indirect(ci_l[:])
        )
        for r in range(4):
            queue = nc.sync if r % 2 == 0 else nc.scalar
            queue.dma_start(first_scales[r:P:32, :].bitcast(I32), picked_bytes[8 * r : P : 32, :].bitcast(I32))

        ci_words = keep.tile([P, H], U32, name="ci_words", tag="ci_words", align_bytes=64)
        nc.vector.tensor_copy(ci_words[:].rearrange("p (t m) -> p m t", t=PACK), d_table[:].indirect(ci_l[:]))
        xq_words = keep.tile([P, S], U32, name="xq_words", tag="xq_words", align_bytes=64)
        nc.vector.tensor_copy(xq_words[:], x_table[:].indirect(offs_l[:]))

        s_bank = [psum.tile([P, S], F32, name="s_bank%d" % t) for t in range(PACK)]
        h_bank = [psum.tile([P, S], F32, name="h_bank%d" % t) for t in range(PACK)]
        for t in range(PACK):
            nc.tensor.matmul_mx(
                out=s_bank[t][:],
                lhsT=ci_words[:, P * t : P * (t + 1)].bitcast(FP8X4),
                lhsT_scale=first_scales[:, S + P * t : S + P * (t + 1)],
                rhs=xq_words[:].bitcast(FP8X4),
                rhs_scale=first_scales[:, 0:S],
                start=True,
                stop=True,
            )

        gs_t = load_rowwise(gs, "gs_t", "xq_words")
        sl_t = load_rowwise(sl, "sl_t", "ci_words")
        th_t = load_rowwise(th, "th_t", "first_scales")

        h_and_s = [keep.tile([P, 2 * S], F32, name="h_and_s%d" % t) for t in range(PACK)]
        pa = keep.tile([P, PACK, W], F32, name="pa")
        pb = keep.tile([P, PACK, W], F32, name="pb")
        rb = keep.tile([P, PACK, W], F32, name="rb")
        ra = keep.tile([P, PACK, W], F32, name="ra")
        flipped = keep.tile([P, PACK, W], F32, name="flipped")
        denom = keep.tile([P, PACK, W], F32, name="denom", tag="denom", align_bytes=64)
        inverse = keep.tile([P, PACK, W], F32, name="inverse")
        dt = [keep.tile([P, S], F32, name="dt%d" % t) for t in range(PACK)]
        z_bf16 = keep.tile([P, S, PACK], BF16, name="z_bf16", align_bytes=64)

        for t in range(PACK):
            s_t = h_and_s[t][:, S : 2 * S]
            if t < 2:
                nc.scalar.activation(s_t, s_bank[t][:], ACT.Copy, scale=0.0625)
            else:
                nc.vector.tensor_scalar(s_t, s_bank[t][:], 0.0625, None, ALU.mult)
            nc.scalar.activation(pb[:, t, :], s_t.indirect(n2_l[:]), ACT.Copy)
            nc.scalar.activation(pa[:, t, :], s_t.indirect(n1_l[:]), ACT.Copy)

        k1_picked_bytes = keep.tile([P, H], U8, name="k1_picked_bytes")
        k1_scales = keep.tile([P, H], U8, name="k1_scales", tag="picked_bytes", align_bytes=64)
        nc.vector.tensor_copy(k1_picked_bytes[:], d_bytes[:].indirect(k1_l[:]))

        nc.vector.tensor_copy(
            k1_scales[:].rearrange("p (t m) -> p t m", t=PACK),
            k1_picked_bytes[:].rearrange("p (m t) -> p t m", t=PACK),
        )
        for r in (1, 2, 3):
            nc.sync.dma_start(k1_scales[r:P:32, :].bitcast(I32), k1_scales[8 * r : P : 32, :].bitcast(I32))
        for pair in (slice(0, 2), slice(2, 4)):
            nc.vector.tensor_tensor(rb[:, pair, :], pa[:, pair, :], pb[:, pair, :], ALU.max)
            nc.vector.tensor_scalar(flipped[:, pair, :], pb[:, pair, :], -1.0, 0.5, ALU.mult, ALU.add)
            nc.vector.scalar_tensor_tensor(denom[:, pair, :], pb[:, pair, :], 0.5, flipped[:, pair, :], ALU.add, ALU.max)
        for t in range(PACK):
            nc.scalar.activation(dt[t][:].indirect(n2_l[:]), rb[:, t, :], ACT.Copy)

        k1_picked = keep.tile([P, H], U32, name="k1_picked", tag="x_table")
        k1_words = keep.tile([P, H], U32, name="k1_words", tag="denom", align_bytes=64)
        bias = keep.tile([P, PACK], F32, name="bias")

        halves = [slice(0, S // 2), slice(S // 2, S)]

        def round_z(t):
            nc.vector.tensor_scalar(z_bf16[:, :, t], dt[t][:], gs_t[:, t : t + 1], None, ALU.mult)

        for t in range(PACK):
            nc.vector.reciprocal(inverse[:, t, :], denom[:, t, :])
            if t > 0:
                nc.gpsimd.tensor_tensor(ra[:, t - 1, :], pa[:, t - 1, :], inverse[:, t - 1, :], ALU.mult)
                nc.scalar.activation(dt[t - 1][:].indirect(n1_l[:]), ra[:, t - 1, :], ACT.Copy)
        nc.vector.scalar_tensor_tensor(bias[:], sl_t[:], -1.0, th_t[:], ALU.mult, ALU.mult)
        nc.gpsimd.tensor_tensor(ra[:, PACK - 1, :], pa[:, PACK - 1, :], inverse[:, PACK - 1, :], ALU.mult)
        nc.scalar.activation(dt[PACK - 1][:].indirect(n1_l[:]), ra[:, PACK - 1, :], ACT.Copy)
        nc.vector.tensor_copy(k1_picked[:], d_table[:].indirect(k1_l[:]))
        nc.vector.tensor_copy(
            k1_words[:].bitcast(I32).rearrange("p (t c i) -> p c t i", t=PACK, i=4),
            k1_picked[:].bitcast(I32).rearrange("p (c i t) -> p c t i", t=PACK, i=4),
        )
        for t in range(PACK - 1):
            round_z(t)
        for half in halves:
            nc.vector.tensor_scalar(z_bf16[:, half, PACK - 1], dt[PACK - 1][:, half], gs_t[:, PACK - 1 : PACK], None, ALU.mult)

        z_words = keep.tile([P, S], U32, name="z_words", align_bytes=64)
        z_scales = keep.tile([P, S], U8, name="z_scales", align_bytes=64)
        for half in halves:
            nc.vector.quantize_mx(
                out=z_words[:, half].bitcast(FP8X4),
                scales=z_scales[:, half],
                in_=z_bf16[:, half, :].rearrange("p j t -> p (j t)"),
            )
        for t in range(PACK):
            for half in halves:
                nc.tensor.matmul_mx(
                    out=h_bank[t][:, half],
                    lhsT=k1_words[:, P * t : P * (t + 1)].bitcast(FP8X4),
                    lhsT_scale=k1_scales[:, P * t : P * (t + 1)],
                    rhs=z_words[:, half].bitcast(FP8X4),
                    rhs_scale=z_scales[:, half],
                    start=True,
                    stop=True,
                )

        st_and_sg = [keep.tile([P, 2 * S], F32, name="st_and_sg%d" % t) for t in range(PACK)]
        fetched = keep.tile([P, PACK, S], F32, name="fetched")
        result = keep.tile([P, PACK, S], F32, name="result")
        result_bf16 = keep.tile([P, S, PACK], BF16, name="result_bf16", align_bytes=64)
        out_rows = out_0.rearrange("(p t) j -> p t j", t=PACK)

        for t in range(PACK):
            nc.vector.tensor_scalar(h_and_s[t][:, 0:S], h_bank[t][:], 0.0625, None, ALU.mult)

        def gate(t):
            nc.scalar.activation(
                st_and_sg[t][:, S : 2 * S],
                h_and_s[t][:].indirect(n3_l[:]),
                ACT.Sigmoid,
                bias=bias[:, t : t + 1],
                scale=sl_t[:, t : t + 1],
            )
            nc.vector.tensor_tensor(st_and_sg[t][:, 0:S], h_and_s[t][:, 0:S], st_and_sg[t][:, S : 2 * S], ALU.mult)

        def finish(t):
            nc.scalar.activation(fetched[:, t, :], st_and_sg[t][:].indirect(n4_l[:]), ACT.Copy)
            nc.vector.scalar_tensor_tensor(
                result[:, t, :], fetched[:, t, :], -0.5, st_and_sg[t][:, 0:S], ALU.mult, ALU.add
            )
            nc.sync.dma_start(out_rows[:, t, :], result[:, t, :])
            if t % 2 == 1:
                nc.vector.tensor_copy(
                    result_bf16[:, :, t - 1 : t + 1], result[:, t - 1 : t + 1, :].rearrange("p t j -> p j t")
                )

        gate(0)
        for t in range(1, PACK):
            gate(t)
            finish(t - 1)

        out_words = keep.tile([P, S], U32, name="out_words", align_bytes=64)
        out_scales = keep.tile([P, S], U8, name="out_scales", align_bytes=64)
        last = PACK - 1
        for half in halves:
            entries = n4_l[:, half.start // 16 : half.stop // 16]
            nc.scalar.activation(fetched[:, last, half], st_and_sg[last][:].indirect(entries), ACT.Copy)
            nc.vector.scalar_tensor_tensor(
                result[:, last, half], fetched[:, last, half], -0.5, st_and_sg[last][:, half], ALU.mult, ALU.add
            )
        for half in halves:
            nc.vector.tensor_copy(
                result_bf16[:, half, last - 1 : last + 1], result[:, last - 1 : last + 1, half].rearrange("p t j -> p j t")
            )
        for half in halves:
            nc.vector.quantize_mx(
                out=out_words[:, half].bitcast(FP8X4),
                scales=out_scales[:, half],
                in_=result_bf16[:, half, :].rearrange("p j t -> p (j t)"),
            )
        nc.sync.dma_start(out_rows[:, last, :], result[:, last, :])
        nc.sync.dma_start(out_1[0].rearrange("p n t -> p (n t)").bitcast(I32), out_words[:].bitcast(I32))
        for q in range(4):
            queue = nc.scalar if q % 2 == 0 else nc.sync
            queue.dma_start(out_2[0][4 * q : 4 * q + 4, :].bitcast(I32), out_scales[32 * q : 32 * q + 4, :].bitcast(I32))
